import numpy as np
import ml_dtypes


def mxq(x, axis, fmt="e4m3"):
    dtype, down = {"e4m3": (ml_dtypes.float8_e4m3fn, 7), "e5m2": (ml_dtypes.float8_e5m2, 14)}[fmt]
    v = np.moveaxis(np.asarray(x, np.float32).astype(ml_dtypes.bfloat16).astype(np.float64), axis, -1)
    blocks = v.reshape(v.shape[:-1] + (-1, 32))
    amax = np.abs(blocks).max(-1, keepdims=True)
    byte = np.maximum(np.where(amax > 0, np.frexp(amax)[1] - 1 + 127, 0) - down, 1)
    scale = np.exp2(byte - 127.0)
    codes = (blocks / scale).astype(np.float32).astype(dtype).astype(np.float64)
    return np.moveaxis((codes * scale).reshape(v.shape), -1, axis)


WIDE = False


def mx_kscale(k):
    if not WIDE:
        return np.ones(k)
    levels = np.array([10, -10, 5, -5, 0])
    if k % 512:
        return np.exp2(np.random.permutation(np.resize(levels, k // 32))).repeat(32)
    a = np.empty((k // 512, 16))
    for p in range(k // 512):
        a[p, :8] = np.random.permutation(np.resize(levels, 8))
        for g in range(8):
            far = levels[np.abs(levels - a[p, g]) >= 10]
            a[p, g + 8] = far[np.random.randint(len(far))]
    return np.exp2(a.ravel()).repeat(32)


def f64(x):
    return np.asarray(x).astype(np.float64)


def striped(idx):
    return np.tile(idx.reshape(-1, 16).T, (8, 1)).astype(np.uint16)


def unstriped(offs):
    return offs[:16].T.reshape(-1).astype(np.int64)


E2M1 = np.array([0.0, 0.5, 1.0, 1.5, 2.0, 3.0, 4.0, 6.0, -0.0, -0.5, -1.0, -1.5, -2.0, -3.0, -4.0, -6.0])


def pack_weight(w, fmt):
    k, n = w.shape
    w = f64(np.asarray(w, np.float32).astype(ml_dtypes.bfloat16)).reshape(k // 32, 32, n)
    amax = np.abs(w).max(1)
    if fmt == "e4m3":
        byte = np.frexp(amax)[1] - 1 + 127 - 7
    else:
        mant, ex = np.frexp(amax / 6.0)
        byte = np.where(mant > 0.5, ex, ex - 1) + 127
    byte = np.clip(np.where(amax > 0, byte, 1), 1, 254)
    scaled = (w * np.exp2(127.0 - byte)[:, None, :]).reshape(k, n).astype(np.float32)
    by_word = np.ascontiguousarray(scaled.reshape(k // 512, 128, 4, n).transpose(0, 1, 3, 2))
    if fmt == "e4m3":
        words = by_word.astype(ml_dtypes.float8_e4m3fn).view(np.uint8)
    else:
        c = by_word.astype(ml_dtypes.float4_e2m1fn).view(np.uint8) & 0xF
        words = (c[..., 0::2] | (c[..., 1::2] << 4)).reshape(k // 512, 128, 2 * n)
    return np.ascontiguousarray(words), np.ascontiguousarray(byte.astype(np.uint8).reshape(k // 512, 16, n))


def unpack_weight(words, scales, fmt):
    g, _, n = scales.shape
    words = np.ascontiguousarray(words).reshape(g, 128, n, -1)
    if fmt == "e4m3":
        vals = words.view(ml_dtypes.float8_e4m3fn).astype(np.float64)
    else:
        nib = np.empty((g, 128, n, 4), np.uint8)
        nib[..., 0::2] = words & 0xF
        nib[..., 1::2] = words >> 4
        vals = E2M1[nib]
    vals = vals * np.repeat(np.exp2(scales.astype(np.float64) - 127.0), 8, axis=1)[..., None]
    return vals.transpose(0, 1, 3, 2).reshape(g * 512, n)


def relu(v):
    return np.maximum(v, 0.0)


K, T, E, C, N = 512, 512, 6, 256, 512
TOP = 3
M = 128


def by_expert(wq, xq):
    return np.concatenate([wq[e].T @ xq[:, e * C:(e + 1) * C] for e in range(E)], axis=1)


def setup_inputs():
    n = np.random.standard_normal
    s = mx_kscale(K)[:, None]
    v = mx_kscale(N)
    deal = np.repeat(np.arange(E), C).reshape(TOP, T)[:, np.random.permutation(T)]
    deal = np.take_along_axis(deal, np.argsort(np.random.rand(TOP, T), axis=0), axis=0)
    for _ in range(8):
        s_, t_ = np.random.permutation(T).reshape(2, -1); r = np.random.randint(TOP, size=T // 2); x, y = deal[r, s_].copy(), deal[r, t_].copy()
        ok = ~((deal[:, s_] == y).any(0) | (deal[:, t_] == x).any(0)); deal[r[ok], s_[ok]] = y[ok]; deal[r[ok], t_[ok]] = x[ok]
    order = np.lexsort((np.random.rand(TOP * T), deal.reshape(-1)))
    slot_token = order % T; pos = np.empty(TOP * T, np.int64); pos[order] = np.arange(TOP * T); pos = pos.reshape(TOP, T)
    g = np.random.uniform(0.5, 1.5, (TOP, T)); g = g / g.sum(0)
    w = [pack_weight(m, "e2m1") for m in n((E, K, N)) / np.sqrt(K) / s[None] * v[None, None, :]]
    x = pack_weight(n((K, T)) * s, "e4m3")
    return {
        "x_words": x[0],
        "x_scales": x[1],
        "w_words": np.stack([m[0] for m in w]),
        "w_scales": np.stack([m[1] for m in w]),
        "b": (0.3 * n((N, E)) * v[:, None]).astype(np.float32),
        "wp": (n((N, M)) / np.sqrt(N) / v[:, None]).astype(np.float32),
        "gate": np.stack([np.tile(r, (N, 1)) for r in g]).astype(np.float32),
        "offs": striped(slot_token),
        "pos1": striped(pos[0]),
        "pos2": striped(pos[1]),
        "pos3": striped(pos[2]),
    }


def reference(x_words, x_scales, w_words, w_scales, b, wp, gate, offs, pos1, pos2, pos3):
    idx = unstriped(offs)
    w = np.stack([unpack_weight(w_words[e], w_scales[e], "e2m1") for e in range(E)])
    xq = unpack_weight(x_words, x_scales, "e4m3")[:, idx]
    y = by_expert(w, xq)
    y = relu(y + np.repeat(f64(b), C, axis=1))
    c = f64(gate[0]) * y[:, unstriped(pos1)] + f64(gate[1]) * y[:, unstriped(pos2)] + f64(gate[2]) * y[:, unstriped(pos3)]
    return mxq(f64(wp), 0, "e4m3").T @ mxq(c, 0, "e4m3")

@@ -1,0 +1,154 @@
+from contextlib import ExitStack
+
+import concourse.mybir as mybir
+from concourse.masks import make_identity
+
+K, T, E, C, N, M, TOP = 512, 512, 6, 256, 512, 128, 3
+S = E * C
+FLOPS = 2 * K * N * S + 2 * N * M * T
+BYTES = K * T + 16 * T + E * (K * N // 2 + 16 * N) + 4 * N * E + 4 * N * M + 4 * TOP * T + 2 * 128 * (S + TOP * T) // 16 + 4 * M * T
+
+F32 = mybir.dt.float32
+BF16 = mybir.dt.bfloat16
+I32 = mybir.dt.int32
+U32 = mybir.dt.uint32
+U16 = mybir.dt.uint16
+U8 = mybir.dt.uint8
+FP8X4 = mybir.dt.float8_e4m3fn_x4
+FP4X4 = mybir.dt.float4_e2m1fn_x4
+ACT = mybir.ActivationFunctionType
+ALU = mybir.AluOpType
+
+P = 128
+NB = N // P
+HALF = T // 2
+TB = HALF // P
+
+
+def tile_moe_nxt_lin_relu_kernel(
+    tc, x_words, x_scales, w_words, w_scales, b, wp, gate, offs, pos1, pos2, pos3, out
+):
+    nc = tc.nc
+    with ExitStack() as ctx:
+        keep = ctx.enter_context(tc.tile_pool(name="keep", bufs=1))
+        ring = ctx.enter_context(tc.tile_pool(name="ring", bufs=2))
+        acc = ctx.enter_context(tc.psum_pool(name="acc", bufs=4))
+        sums = ctx.enter_context(tc.psum_pool(name="sums", bufs=3))
+        last = ctx.enter_context(tc.psum_pool(name="last", bufs=1))
+
+        xw = keep.tile([P, T], I32, align_bytes=64)
+        offs_sb = keep.tile([P, S // 16], U16)
+        xs = keep.tile([P, T], U8, align_bytes=64)
+        ws = keep.tile([P, E, N], U8, align_bytes=64)
+        w_a = keep.tile([P, 2, 2 * N], U8, align_bytes=64)
+        w_b = keep.tile([P, E - 2, 2 * N], U8, align_bytes=64)
+        b_sb = keep.tile([P, NB, E], F32)
+        wp_raw = keep.tile([P, 4, M], F32)
+        g_sb = keep.tile([P, TOP * T // P], F32)
+        pos_sb = [keep.tile([P, T // 16], U16, name="pos%d" % s) for s in range(TOP)]
+        ident = keep.tile([P, P], F32)
+        warm = keep.tile([P, 2], F32)
+
+        nc.vector.memset(xs[:].bitcast(I32), 0)
+        nc.vector.memset(warm[:], 0.0)
+        nc.vector.memset(ws[:].rearrange("p e n -> p (e n)").bitcast(I32), 0)
+        nc.scalar.activation(warm[:, 1:2], warm[:, 0:1], ACT.Relu)
+
+        nc.sync.dma_start(xw[:], x_words[0].rearrange("p t r -> p (t r)").bitcast(I32))
+        nc.sync.dma_start(b_sb[:], b.rearrange("(j m) e -> m j e", m=P))
+        for r in range(4):
+            nc.sync.dma_start(xs[r:P:32, :].bitcast(I32), x_scales[0, r:16:4, :].bitcast(I32))
+        nc.sync.dma_start(offs_sb[:], offs)
+        for r in range(4):
+            nc.sync.dma_start(
+                ws[r:P:32, :, :].bitcast(I32),
+                w_scales[:, 0, r:16:4, :].rearrange("e q n -> q e n").bitcast(I32),
+            )
+        nc.sync.dma_start(w_a[:].bitcast(I32), w_words[0:2, 0].rearrange("e p c -> p e c").bitcast(I32))
+        nc.sync.dma_start(w_b[:].bitcast(I32), w_words[2:E, 0].rearrange("e p c -> p e c").bitcast(I32))
+        for s, pos in enumerate((pos1, pos2, pos3)):
+            nc.sync.dma_start(pos_sb[s][:], pos)
+        nc.sync.dma_start(wp_raw[:], wp.rearrange("(q r) f -> q r f", r=4))
+        gate_rows = gate.rearrange("s n (u p) -> (s n u) p", p=P)
+        with nc.allow_non_contiguous_dma(reason="one gate value a partition"):
+            nc.sync.dma_start(g_sb[:], gate_rows[0 : 11 * 513 + 1 : 513, :].rearrange("u p -> p u"))
+        make_identity(nc, ident[:])
+
+        xg = keep.tile([P, S], U32, align_bytes=64)
+        xsg = keep.tile([P, S], U8, align_bytes=64)
+        y = [keep.tile([P, S], F32, name="y%d" % j) for j in range(NB)]
+
+        def expert_block(e, j):
+            slots = slice(e * C, (e + 1) * C)
+            words = w_a[:, e, :] if e < 2 else w_b[:, e - 2, :]
+            z = acc.tile([P, C], F32, name="acc")
+            nc.tensor.matmul_mx(
+                out=z[:],
+                lhsT=words[:, 2 * P * j : 2 * P * (j + 1)].bitcast(FP4X4),
+                lhsT_scale=ws[:, e, P * j : P * (j + 1)],
+                rhs=xg[:, slots].bitcast(FP8X4),
+                rhs_scale=xsg[:, slots],
+                start=True,
+                stop=True,
+            )
+            nc.scalar.activation(y[j][:, slots], z[:], ACT.Relu, bias=b_sb[:, j, e : e + 1])
+
+        for e in range(E):
+            slots = slice(e * C, (e + 1) * C)
+            picks = offs_sb[:, e * C // 16 : (e + 1) * C // 16]
+            nc.vector.tensor_copy(xg[:, slots], xw[:].bitcast(U32).indirect(picks))
+            nc.vector.tensor_copy(xsg[:, slots], xs[:].indirect(picks))
+            for j in range(NB):
+                expert_block(e, j)
+
+        wp_bf = keep.tile([P, M, 4], BF16, align_bytes=64)
+        wq = keep.tile([P, M], U32, align_bytes=64)
+        wq_s = keep.tile([P, M], U8, align_bytes=64)
+        nc.vector.tensor_copy(wp_bf[:], wp_raw[:].rearrange("q r f -> q f r"))
+        nc.vector.quantize_mx(out=wq[:].bitcast(FP8X4), scales=wq_s[:], in_=wp_bf[:].rearrange("q f r -> q (f r)"))
+
+        for h in range(2):
+            csum = [sums.tile([P, 4, P], F32, name="csum") for tb in range(TB)]
+            for s in range(TOP):
+                picks = pos_sb[s][:, h * HALF // 16 : (h + 1) * HALF // 16]
+                turned = [acc.tile([P, N], F32, name="acc") for tb in range(TB)]
+                for j in range(NB):
+                    got = ring.tile([P, HALF], F32, name="got%d" % j)
+                    nc.vector.tensor_copy(got[:], y[j][:].indirect(picks))
+                    for tb in range(TB):
+                        nc.tensor.transpose(turned[tb][:, P * j : P * (j + 1)], got[:, P * tb : P * (tb + 1)], ident[:])
+                for tb in range(TB):
+                    u = 4 * s + TB * h + tb
+                    gated = keep.tile([P, 4, P], F32, name="gated%d" % u)
+                    view = turned[tb][:].rearrange("t (q r) -> t r q", r=4)
+                    if h == 1 and s == TOP - 1 and tb == TB - 1:
+                        nc.vector.tensor_scalar(gated[:], view, g_sb[:, u : u + 1], None, ALU.mult)
+                    else:
+                        nc.scalar.activation(gated[:], view, ACT.Copy, scale=g_sb[:, u : u + 1])
+                    for r in range(4):
+                        nc.tensor.matmul(
+                            csum[tb][:, r, :],
+                            lhsT=gated[:, r, :],
+                            rhs=ident[:],
+                            is_transpose=True,
+                            start=(s == 0 and r == 0),
+                            stop=(s == TOP - 1 and r == 3),
+                        )
+            c_bf = keep.tile([P, HALF, 4], BF16, align_bytes=64, name="c_bf%d" % h)
+            for tb in range(TB):
+                view = csum[tb][:].rearrange("q r t -> q t r")
+                if h == 1 and tb == TB - 1:
+                    nc.vector.tensor_copy(c_bf[:, P * tb : P * (tb + 1), :], view)
+                else:
+                    nc.scalar.copy(c_bf[:, P * tb : P * (tb + 1), :], view)
+            cq = keep.tile([P, HALF], U32, align_bytes=64, name="cq%d" % h)
+            cq_s = keep.tile([P, HALF], U8, align_bytes=64, name="cq_s%d" % h)
+            nc.vector.quantize_mx(out=cq[:].bitcast(FP8X4), scales=cq_s[:], in_=c_bf[:].rearrange("q t r -> q (t r)"))
+            proj = last.tile([P, HALF], F32, name="proj")
+            nc.tensor.matmul_mx(
+                out=proj[:], lhsT=wq[:].bitcast(FP8X4), lhsT_scale=wq_s[:], rhs=cq[:].bitcast(FP8X4), rhs_scale=cq_s[:],
+                start=True, stop=True,
+            )
+            o_sb = keep.tile([P, HALF], F32, name="o_sb%d" % h)
+            nc.scalar.copy(o_sb[:], proj[:])
+            nc.sync.dma_start(out[:, h * HALF : (h + 1) * HALF], o_sb[:])

@@ -23,6 +23,8 @@ P = 128
 NB = N // P
 HALF = T // 2
 TB = HALF // P
+BANK = 2048
+W_GROUPS = ((0, 1), (1, 3), (3, 6))
 
 
 def tile_moe_nxt_lin_relu_kernel(
@@ -32,16 +34,15 @@ def tile_moe_nxt_lin_relu_kernel(
     with ExitStack() as ctx:
         keep = ctx.enter_context(tc.tile_pool(name="keep", bufs=1))
         ring = ctx.enter_context(tc.tile_pool(name="ring", bufs=2))
-        acc = ctx.enter_context(tc.psum_pool(name="acc", bufs=4))
-        sums = ctx.enter_context(tc.psum_pool(name="sums", bufs=3))
-        last = ctx.enter_context(tc.psum_pool(name="last", bufs=1))
+        psum = ctx.enter_context(tc.psum_pool(name="psum", bufs=1))
 
         xw = keep.tile([P, T], I32, align_bytes=64)
         offs_sb = keep.tile([P, S // 16], U16)
         xs = keep.tile([P, T], U8, align_bytes=64)
         ws = keep.tile([P, E, N], U8, align_bytes=64)
-        w_a = keep.tile([P, 2, 2 * N], U8, align_bytes=64)
-        w_b = keep.tile([P, E - 2, 2 * N], U8, align_bytes=64)
+        w_sb = [
+            keep.tile([P, stop - first, 2 * N], U8, align_bytes=64, name="w%d" % first) for first, stop in W_GROUPS
+        ]
         b_sb = keep.tile([P, NB, E], F32)
         wp_raw = keep.tile([P, 4, M], F32)
         g_sb = keep.tile([P, TOP * T // P], F32)
@@ -54,18 +55,23 @@ def tile_moe_nxt_lin_relu_kernel(
         nc.vector.memset(ws[:].rearrange("p e n -> p (e n)").bitcast(I32), 0)
         nc.scalar.activation(warm[:, 1:2], warm[:, 0:1], ACT.Relu)
 
+        def load_words(g):
+            first, stop = W_GROUPS[g]
+            nc.sync.dma_start(w_sb[g][:].bitcast(I32), w_words[first:stop, 0].rearrange("e p c -> p e c").bitcast(I32))
+
         nc.sync.dma_start(xw[:], x_words[0].rearrange("p t r -> p (t r)").bitcast(I32))
+        nc.sync.dma_start(offs_sb[:], offs)
         nc.sync.dma_start(b_sb[:], b.rearrange("(j m) e -> m j e", m=P))
+        load_words(0)
         for r in range(4):
             nc.sync.dma_start(xs[r:P:32, :].bitcast(I32), x_scales[0, r:16:4, :].bitcast(I32))
-        nc.sync.dma_start(offs_sb[:], offs)
         for r in range(4):
             nc.sync.dma_start(
                 ws[r:P:32, :, :].bitcast(I32),
                 w_scales[:, 0, r:16:4, :].rearrange("e q n -> q e n").bitcast(I32),
             )
-        nc.sync.dma_start(w_a[:].bitcast(I32), w_words[0:2, 0].rearrange("e p c -> p e c").bitcast(I32))
-        nc.sync.dma_start(w_b[:].bitcast(I32), w_words[2:E, 0].rearrange("e p c -> p e c").bitcast(I32))
+        load_words(1)
+        load_words(2)
         for s, pos in enumerate((pos1, pos2, pos3)):
             nc.sync.dma_start(pos_sb[s][:], pos)
         nc.sync.dma_start(wp_raw[:], wp.rearrange("(q r) f -> q r f", r=4))
@@ -74,32 +80,49 @@ def tile_moe_nxt_lin_relu_kernel(
             nc.sync.dma_start(g_sb[:], gate_rows[0 : 11 * 513 + 1 : 513, :].rearrange("u p -> p u"))
         make_identity(nc, ident[:])
 
-        xg = keep.tile([P, S], U32, align_bytes=64)
         xsg = keep.tile([P, S], U8, align_bytes=64)
         y = [keep.tile([P, S], F32, name="y%d" % j) for j in range(NB)]
+        xg = {}
+        z = {}
+
+        def gather_tokens(e):
+            picks = offs_sb[:, e * C // 16 : (e + 1) * C // 16]
+            xg[e] = ring.tile([P, C], U32, align_bytes=64, name="xg", bufs=3)
+            nc.vector.tensor_copy(xg[e][:], xw[:].bitcast(U32).indirect(picks))
+            nc.vector.tensor_copy(xsg[:, e * C : (e + 1) * C], xs[:].indirect(picks))
 
         def expert_block(e, j):
             slots = slice(e * C, (e + 1) * C)
-            words = w_a[:, e, :] if e < 2 else w_b[:, e - 2, :]
-            z = acc.tile([P, C], F32, name="acc")
+            g = [first <= e < stop for first, stop in W_GROUPS].index(True)
+            words = w_sb[g][:, e - W_GROUPS[g][0], :]
+            z[e, j] = psum.tile([P, C], F32, name="z%d_%d" % (e, j), offset=((NB * e + j) % 8) * BANK)
             nc.tensor.matmul_mx(
-                out=z[:],
+                out=z[e, j][:],
                 lhsT=words[:, 2 * P * j : 2 * P * (j + 1)].bitcast(FP4X4),
                 lhsT_scale=ws[:, e, P * j : P * (j + 1)],
-                rhs=xg[:, slots].bitcast(FP8X4),
+                rhs=xg[e][:].bitcast(FP8X4),
                 rhs_scale=xsg[:, slots],
                 start=True,
                 stop=True,
             )
-            nc.scalar.activation(y[j][:, slots], z[:], ACT.Relu, bias=b_sb[:, j, e : e + 1])
+
+        def finish_block(e, j):
+            slots = slice(e * C, (e + 1) * C)
+            if e == E - 1 and j == 0:
+                nc.vector.tensor_scalar(y[j][:, slots], z[e, j][:], b_sb[:, j, e : e + 1], 0.0, ALU.add, ALU.max)
+            else:
+                nc.scalar.activation(y[j][:, slots], z[e, j][:], ACT.Relu, bias=b_sb[:, j, e : e + 1])
 
         for e in range(E):
-            slots = slice(e * C, (e + 1) * C)
-            picks = offs_sb[:, e * C // 16 : (e + 1) * C // 16]
-            nc.vector.tensor_copy(xg[:, slots], xw[:].bitcast(U32).indirect(picks))
-            nc.vector.tensor_copy(xsg[:, slots], xs[:].indirect(picks))
+            gather_tokens(e)
             for j in range(NB):
                 expert_block(e, j)
+            if e < E - 2:
+                for j in range(NB):
+                    finish_block(e, j)
+        for j in range(NB):
+            finish_block(E - 2, j)
+            finish_block(E - 1, j)
 
         wp_bf = keep.tile([P, M, 4], BF16, align_bytes=64)
         wq = keep.tile([P, M], U32, align_bytes=64)
@@ -107,48 +130,78 @@ def tile_moe_nxt_lin_relu_kernel(
         nc.vector.tensor_copy(wp_bf[:], wp_raw[:].rearrange("q r f -> q f r"))
         nc.vector.quantize_mx(out=wq[:].bitcast(FP8X4), scales=wq_s[:], in_=wp_bf[:].rearrange("q f r -> q (f r)"))
 
-        for h in range(2):
-            csum = [sums.tile([P, 4, P], F32, name="csum") for tb in range(TB)]
-            for s in range(TOP):
-                picks = pos_sb[s][:, h * HALF // 16 : (h + 1) * HALF // 16]
-                turned = [acc.tile([P, N], F32, name="acc") for tb in range(TB)]
-                for j in range(NB):
-                    got = ring.tile([P, HALF], F32, name="got%d" % j)
-                    nc.vector.tensor_copy(got[:], y[j][:].indirect(picks))
-                    for tb in range(TB):
-                        nc.tensor.transpose(turned[tb][:, P * j : P * (j + 1)], got[:, P * tb : P * (tb + 1)], ident[:])
+        csum = {}
+
+        def combine(h, s):
+            if s == 0:
                 for tb in range(TB):
-                    u = 4 * s + TB * h + tb
-                    gated = keep.tile([P, 4, P], F32, name="gated%d" % u)
-                    view = turned[tb][:].rearrange("t (q r) -> t r q", r=4)
-                    if h == 1 and s == TOP - 1 and tb == TB - 1:
-                        nc.vector.tensor_scalar(gated[:], view, g_sb[:, u : u + 1], None, ALU.mult)
-                    else:
-                        nc.scalar.activation(gated[:], view, ACT.Copy, scale=g_sb[:, u : u + 1])
-                    for r in range(4):
-                        nc.tensor.matmul(
-                            csum[tb][:, r, :],
-                            lhsT=gated[:, r, :],
-                            rhs=ident[:],
-                            is_transpose=True,
-                            start=(s == 0 and r == 0),
-                            stop=(s == TOP - 1 and r == 3),
-                        )
-            c_bf = keep.tile([P, HALF, 4], BF16, align_bytes=64, name="c_bf%d" % h)
-            for tb in range(TB):
-                view = csum[tb][:].rearrange("q r t -> q t r")
-                if h == 1 and tb == TB - 1:
-                    nc.vector.tensor_copy(c_bf[:, P * tb : P * (tb + 1), :], view)
+                    bank = 4 + TB * h + tb
+                    csum[h, tb] = psum.tile([P, 4, P], F32, name="csum%d" % bank, offset=bank * BANK)
+            picks = pos_sb[s][:, h * HALF // 16 : (h + 1) * HALF // 16]
+            stage = TOP * h + s
+            final = stage == 2 * TOP - 1
+            turned = psum.tile([P, TB, N], F32, name="turned%d" % stage, offset=(2 * (stage + 1) % 4) * BANK)
+            late = psum.tile([P, TB, N], F32, name="late", offset=(2 * stage % 4) * BANK) if final else turned
+            for j in range(NB):
+                if final and j == 2:
+                    got = keep.tile([P, HALF], F32, align_bytes=64, name="c_bf0")
                 else:
-                    nc.scalar.copy(c_bf[:, P * tb : P * (tb + 1), :], view)
-            cq = keep.tile([P, HALF], U32, align_bytes=64, name="cq%d" % h)
-            cq_s = keep.tile([P, HALF], U8, align_bytes=64, name="cq_s%d" % h)
+                    got = keep.tile([P, HALF], F32, name="got%d" % j)
+                nc.vector.tensor_copy(got[:], y[j][:].indirect(picks))
+                dest = late if j == NB - 1 else turned
+                for tb in range(TB):
+                    nc.tensor.transpose(dest[:, tb, P * j : P * (j + 1)], got[:, P * tb : P * (tb + 1)], ident[:])
+            for tb in range(TB):
+                u = 4 * s + TB * h + tb
+                gated = keep.tile([P, 4, P], F32, name="gated%d" % u)
+                weight = g_sb[:, u : u + 1]
+                if final:
+                    view = turned[:, tb, : 3 * P].rearrange("t (q r) -> t r q", r=4)
+                    nc.scalar.activation(gated[:, :, :96], view, ACT.Copy, scale=weight)
+                    view = late[:, tb, 3 * P :].rearrange("t (q r) -> t r q", r=4)
+                    nc.vector.tensor_scalar(gated[:, :, 96:], view, weight, None, ALU.mult)
+                else:
+                    view = turned[:, tb, :].rearrange("t (q r) -> t r q", r=4)
+                    nc.scalar.activation(gated[:], view, ACT.Copy, scale=weight)
+                for r in range(4):
+                    nc.tensor.matmul(
+                        csum[h, tb][:, r, :],
+                        lhsT=gated[:, r, :],
+                        rhs=ident[:],
+                        is_transpose=True,
+                        start=(s == 0 and r == 0),
+                        stop=(s == TOP - 1 and r == 3),
+                    )
+
+        def project(h, blocks, bank):
+            first, width = HALF * h + P * blocks[0], P * len(blocks)
+            c_bf = keep.tile([P, width, 4], BF16, align_bytes=64, name="c_bf%d" % first)
+            for i, tb in enumerate(blocks):
+                view = csum[h, tb][:].rearrange("q r t -> q t r")
+                if h == 1 and tb == 0:
+                    nc.vector.tensor_copy(c_bf[:, P * i : P * (i + 1), :], view)
+                else:
+                    nc.scalar.copy(c_bf[:, P * i : P * (i + 1), :], view)
+            cq = keep.tile([P, width], U32, align_bytes=64, name="cq%d" % first)
+            cq_s = keep.tile([P, width], U8, align_bytes=64, name="cq_s%d" % first)
             nc.vector.quantize_mx(out=cq[:].bitcast(FP8X4), scales=cq_s[:], in_=c_bf[:].rearrange("q t r -> q (t r)"))
-            proj = last.tile([P, HALF], F32, name="proj")
+            proj = psum.tile([P, width], F32, name="proj%d" % first, offset=bank * BANK)
             nc.tensor.matmul_mx(
                 out=proj[:], lhsT=wq[:].bitcast(FP8X4), lhsT_scale=wq_s[:], rhs=cq[:].bitcast(FP8X4), rhs_scale=cq_s[:],
                 start=True, stop=True,
             )
-            o_sb = keep.tile([P, HALF], F32, name="o_sb%d" % h)
-            nc.scalar.copy(o_sb[:], proj[:])
-            nc.sync.dma_start(out[:, h * HALF : (h + 1) * HALF], o_sb[:])
+            o_sb = keep.tile([P, width], F32, name="o_sb%d" % first)
+            if first == T - P:
+                nc.vector.tensor_copy(o_sb[:], proj[:])
+            else:
+                nc.scalar.copy(o_sb[:], proj[:])
+            nc.sync.dma_start(out[:, first : first + width], o_sb[:])
+
+        for s in range(TOP):
+            combine(0, s)
+        combine(1, 0)
+        project(0, (0, 1), 4)
+        for s in range(1, TOP):
+            combine(1, s)
+        project(1, (0,), 5)
+        project(1, (1,), 4)

@@ -24,6 +24,7 @@ NB = N // P
 HALF = T // 2
 TB = HALF // P
 BANK = 2048
+ON_VECTOR = ((4, 0), (4, 1), (5, 0))
 W_GROUPS = ((0, 1), (1, 3), (3, 6))
 
 
@@ -59,9 +60,8 @@ def tile_moe_nxt_lin_relu_kernel(
             first, stop = W_GROUPS[g]
             nc.sync.dma_start(w_sb[g][:].bitcast(I32), w_words[first:stop, 0].rearrange("e p c -> p e c").bitcast(I32))
 
-        nc.sync.dma_start(xw[:], x_words[0].rearrange("p t r -> p (t r)").bitcast(I32))
         nc.sync.dma_start(offs_sb[:], offs)
-        nc.sync.dma_start(b_sb[:], b.rearrange("(j m) e -> m j e", m=P))
+        nc.sync.dma_start(xw[:], x_words[0].rearrange("p t r -> p (t r)").bitcast(I32))
         load_words(0)
         for r in range(4):
             nc.sync.dma_start(xs[r:P:32, :].bitcast(I32), x_scales[0, r:16:4, :].bitcast(I32))
@@ -70,6 +70,7 @@ def tile_moe_nxt_lin_relu_kernel(
                 ws[r:P:32, :, :].bitcast(I32),
                 w_scales[:, 0, r:16:4, :].rearrange("e q n -> q e n").bitcast(I32),
             )
+        nc.sync.dma_start(b_sb[:], b.rearrange("(j m) e -> m j e", m=P))
         load_words(1)
         load_words(2)
         for s, pos in enumerate((pos1, pos2, pos3)):
@@ -87,7 +88,7 @@ def tile_moe_nxt_lin_relu_kernel(
 
         def gather_tokens(e):
             picks = offs_sb[:, e * C // 16 : (e + 1) * C // 16]
-            xg[e] = ring.tile([P, C], U32, align_bytes=64, name="xg", bufs=3)
+            xg[e] = ring.tile([P, C], U32, align_bytes=64, name="xg", bufs=4)
             nc.vector.tensor_copy(xg[e][:], xw[:].bitcast(U32).indirect(picks))
             nc.vector.tensor_copy(xsg[:, e * C : (e + 1) * C], xs[:].indirect(picks))
 
@@ -108,7 +109,7 @@ def tile_moe_nxt_lin_relu_kernel(
 
         def finish_block(e, j):
             slots = slice(e * C, (e + 1) * C)
-            if e == E - 1 and j == 0:
+            if (e, j) in ON_VECTOR:
                 nc.vector.tensor_scalar(y[j][:, slots], z[e, j][:], b_sb[:, j, e : e + 1], 0.0, ALU.add, ALU.max)
             else:
                 nc.scalar.activation(y[j][:, slots], z[e, j][:], ACT.Relu, bias=b_sb[:, j, e : e + 1])
@@ -119,18 +120,17 @@ def tile_moe_nxt_lin_relu_kernel(
                 expert_block(e, j)
             if e < E - 2:
                 for j in range(NB):
-                    finish_block(e, j)
+                    if (e, j) not in ON_VECTOR:
+                        finish_block(e, j)
         for j in range(NB):
             finish_block(E - 2, j)
             finish_block(E - 1, j)
 
-        wp_bf = keep.tile([P, M, 4], BF16, align_bytes=64)
         wq = keep.tile([P, M], U32, align_bytes=64)
         wq_s = keep.tile([P, M], U8, align_bytes=64)
-        nc.vector.tensor_copy(wp_bf[:], wp_raw[:].rearrange("q r f -> q f r"))
-        nc.vector.quantize_mx(out=wq[:].bitcast(FP8X4), scales=wq_s[:], in_=wp_bf[:].rearrange("q f r -> q (f r)"))
 
         csum = {}
+        held = {}
 
         def combine(h, s):
             if s == 0:
@@ -141,29 +141,26 @@ def tile_moe_nxt_lin_relu_kernel(
             stage = TOP * h + s
             final = stage == 2 * TOP - 1
             turned = psum.tile([P, TB, N], F32, name="turned%d" % stage, offset=(2 * (stage + 1) % 4) * BANK)
-            late = psum.tile([P, TB, N], F32, name="late", offset=(2 * stage % 4) * BANK) if final else turned
             for j in range(NB):
                 if final and j == 2:
                     got = keep.tile([P, HALF], F32, align_bytes=64, name="c_bf0")
                 else:
                     got = keep.tile([P, HALF], F32, name="got%d" % j)
                 nc.vector.tensor_copy(got[:], y[j][:].indirect(picks))
-                dest = late if j == NB - 1 else turned
                 for tb in range(TB):
-                    nc.tensor.transpose(dest[:, tb, P * j : P * (j + 1)], got[:, P * tb : P * (tb + 1)], ident[:])
+                    nc.tensor.transpose(turned[:, tb, P * j : P * (j + 1)], got[:, P * tb : P * (tb + 1)], ident[:])
             for tb in range(TB):
                 u = 4 * s + TB * h + tb
-                gated = keep.tile([P, 4, P], F32, name="gated%d" % u)
+                gated = keep.tile([P, 4, P], F32, align_bytes=64, name="gated%d" % u)
                 weight = g_sb[:, u : u + 1]
+                view = turned[:, tb, :].rearrange("t (q r) -> t r q", r=4)
                 if final:
-                    view = turned[:, tb, : 3 * P].rearrange("t (q r) -> t r q", r=4)
-                    nc.scalar.activation(gated[:, :, :96], view, ACT.Copy, scale=weight)
-                    view = late[:, tb, 3 * P :].rearrange("t (q r) -> t r q", r=4)
-                    nc.vector.tensor_scalar(gated[:, :, 96:], view, weight, None, ALU.mult)
+                    nc.vector.scalar_tensor_tensor(gated[:], view, weight, held[tb][:], ALU.mult, ALU.add)
                 else:
-                    view = turned[:, tb, :].rearrange("t (q r) -> t r q", r=4)
                     nc.scalar.activation(gated[:], view, ACT.Copy, scale=weight)
-                for r in range(4):
+                if stage == 2 * TOP - 2:
+                    held[tb] = gated
+                for r in range(0 if stage == 2 * TOP - 2 else 4):
                     nc.tensor.matmul(
                         csum[h, tb][:, r, :],
                         lhsT=gated[:, r, :],
@@ -178,10 +175,7 @@ def tile_moe_nxt_lin_relu_kernel(
             c_bf = keep.tile([P, width, 4], BF16, align_bytes=64, name="c_bf%d" % first)
             for i, tb in enumerate(blocks):
                 view = csum[h, tb][:].rearrange("q r t -> q t r")
-                if h == 1 and tb == 0:
-                    nc.vector.tensor_copy(c_bf[:, P * i : P * (i + 1), :], view)
-                else:
-                    nc.scalar.copy(c_bf[:, P * i : P * (i + 1), :], view)
+                nc.scalar.copy(c_bf[:, P * i : P * (i + 1), :], view)
             cq = keep.tile([P, width], U32, align_bytes=64, name="cq%d" % first)
             cq_s = keep.tile([P, width], U8, align_bytes=64, name="cq_s%d" % first)
             nc.vector.quantize_mx(out=cq[:].bitcast(FP8X4), scales=cq_s[:], in_=c_bf[:].rearrange("q t r -> q (t r)"))
@@ -199,6 +193,9 @@ def tile_moe_nxt_lin_relu_kernel(
 
         for s in range(TOP):
             combine(0, s)
+        wp_bf = keep.tile([P, M, 4], BF16, align_bytes=64, name="gated0")
+        nc.scalar.copy(wp_bf[:], wp_raw[:].rearrange("q r f -> q f r"))
+        nc.vector.quantize_mx(out=wq[:].bitcast(FP8X4), scales=wq_s[:], in_=wp_bf[:].rearrange("q f r -> q (f r)"))
         combine(1, 0)
         project(0, (0, 1), 4)
         for s in range(1, TOP):

@@ -24,6 +24,7 @@ NB = N // P
 HALF = T // 2
 TB = HALF // P
 BANK = 2048
+ORDER = [(e, j) for e in range(E - 2) for j in range(NB)] + [(4, 0), (4, 1), (5, 0), (5, 1), (4, 2), (5, 2), (4, 3), (5, 3)]
 ON_VECTOR = ((4, 0), (4, 1), (5, 0))
 W_GROUPS = ((0, 1), (1, 3), (3, 6))
 
@@ -62,9 +63,9 @@ def tile_moe_nxt_lin_relu_kernel(
 
         nc.sync.dma_start(offs_sb[:], offs)
         nc.sync.dma_start(xw[:], x_words[0].rearrange("p t r -> p (t r)").bitcast(I32))
-        load_words(0)
         for r in range(4):
             nc.sync.dma_start(xs[r:P:32, :].bitcast(I32), x_scales[0, r:16:4, :].bitcast(I32))
+        load_words(0)
         for r in range(4):
             nc.sync.dma_start(
                 ws[r:P:32, :, :].bitcast(I32),
@@ -96,7 +97,7 @@ def tile_moe_nxt_lin_relu_kernel(
             slots = slice(e * C, (e + 1) * C)
             g = [first <= e < stop for first, stop in W_GROUPS].index(True)
             words = w_sb[g][:, e - W_GROUPS[g][0], :]
-            z[e, j] = psum.tile([P, C], F32, name="z%d_%d" % (e, j), offset=((NB * e + j) % 8) * BANK)
+            z[e, j] = psum.tile([P, C], F32, name="z%d_%d" % (e, j), offset=(ORDER.index((e, j)) % 8) * BANK)
             nc.tensor.matmul_mx(
                 out=z[e, j][:],
                 lhsT=words[:, 2 * P * j : 2 * P * (j + 1)].bitcast(FP4X4),
@@ -114,55 +115,44 @@ def tile_moe_nxt_lin_relu_kernel(
             else:
                 nc.scalar.activation(y[j][:, slots], z[e, j][:], ACT.Relu, bias=b_sb[:, j, e : e + 1])
 
-        for e in range(E):
-            gather_tokens(e)
-            for j in range(NB):
-                expert_block(e, j)
-            if e < E - 2:
-                for j in range(NB):
-                    if (e, j) not in ON_VECTOR:
-                        finish_block(e, j)
-        for j in range(NB):
-            finish_block(E - 2, j)
-            finish_block(E - 1, j)
+        for e, j in ORDER:
+            if j == 0 and e < E - 1:
+                gather_tokens(e)
+            if (e, j) == (E - 2, 0):
+                gather_tokens(E - 1)
+            expert_block(e, j)
+            finish_block(e, j)
 
         wq = keep.tile([P, M], U32, align_bytes=64)
         wq_s = keep.tile([P, M], U8, align_bytes=64)
 
-        csum = {}
+        csum = [psum.tile([P, 4, P], F32, name="csum%d" % tb, offset=(2 + tb) * BANK) for tb in range(TB)]
         held = {}
 
-        def combine(h, s):
-            if s == 0:
-                for tb in range(TB):
-                    bank = 4 + TB * h + tb
-                    csum[h, tb] = psum.tile([P, 4, P], F32, name="csum%d" % bank, offset=bank * BANK)
+        def fetch(h, s):
             picks = pos_sb[s][:, h * HALF // 16 : (h + 1) * HALF // 16]
             stage = TOP * h + s
-            final = stage == 2 * TOP - 1
-            turned = psum.tile([P, TB, N], F32, name="turned%d" % stage, offset=(2 * (stage + 1) % 4) * BANK)
+            turned = psum.tile([P, TB, N], F32, name="turned%d" % stage, offset=(0 if stage % 2 else 5) * BANK)
             for j in range(NB):
-                if final and j == 2:
+                if stage == 2 * TOP - 1 and j == 2:
                     got = keep.tile([P, HALF], F32, align_bytes=64, name="c_bf0")
                 else:
                     got = keep.tile([P, HALF], F32, name="got%d" % j)
                 nc.vector.tensor_copy(got[:], y[j][:].indirect(picks))
                 for tb in range(TB):
                     nc.tensor.transpose(turned[:, tb, P * j : P * (j + 1)], got[:, P * tb : P * (tb + 1)], ident[:])
+            return turned
+
+        def combine_first(s):
+            turned = fetch(0, s)
             for tb in range(TB):
-                u = 4 * s + TB * h + tb
+                u = 4 * s + tb
                 gated = keep.tile([P, 4, P], F32, align_bytes=64, name="gated%d" % u)
-                weight = g_sb[:, u : u + 1]
                 view = turned[:, tb, :].rearrange("t (q r) -> t r q", r=4)
-                if final:
-                    nc.vector.scalar_tensor_tensor(gated[:], view, weight, held[tb][:], ALU.mult, ALU.add)
-                else:
-                    nc.scalar.activation(gated[:], view, ACT.Copy, scale=weight)
-                if stage == 2 * TOP - 2:
-                    held[tb] = gated
-                for r in range(0 if stage == 2 * TOP - 2 else 4):
+                nc.scalar.activation(gated[:], view, ACT.Copy, scale=g_sb[:, u : u + 1])
+                for r in range(4):
                     nc.tensor.matmul(
-                        csum[h, tb][:, r, :],
+                        csum[tb][:, r, :],
                         lhsT=gated[:, r, :],
                         rhs=ident[:],
                         is_transpose=True,
@@ -170,12 +160,21 @@ def tile_moe_nxt_lin_relu_kernel(
                         stop=(s == TOP - 1 and r == 3),
                     )
 
-        def project(h, blocks, bank):
-            first, width = HALF * h + P * blocks[0], P * len(blocks)
-            c_bf = keep.tile([P, width, 4], BF16, align_bytes=64, name="c_bf%d" % first)
-            for i, tb in enumerate(blocks):
-                view = csum[h, tb][:].rearrange("q r t -> q t r")
-                nc.scalar.copy(c_bf[:, P * i : P * (i + 1), :], view)
+        def combine_second(s):
+            turned = fetch(1, s)
+            for tb in range(TB):
+                u = 4 * s + TB + tb
+                part = keep.tile([P, N], BF16 if s == TOP - 1 else F32, name="part%d" % u)
+                if s == 0:
+                    nc.scalar.activation(part[:], turned[:, tb, :], ACT.Copy, scale=g_sb[:, u : u + 1])
+                else:
+                    nc.vector.scalar_tensor_tensor(
+                        part[:], turned[:, tb, :], g_sb[:, u : u + 1], held[tb][:], ALU.mult, ALU.add
+                    )
+                held[tb] = part
+
+        def project(c_bf, first, bank):
+            width = c_bf.shape[1]
             cq = keep.tile([P, width], U32, align_bytes=64, name="cq%d" % first)
             cq_s = keep.tile([P, width], U8, align_bytes=64, name="cq_s%d" % first)
             nc.vector.quantize_mx(out=cq[:].bitcast(FP8X4), scales=cq_s[:], in_=c_bf[:].rearrange("q t r -> q (t r)"))
@@ -192,13 +191,25 @@ def tile_moe_nxt_lin_relu_kernel(
             nc.sync.dma_start(out[:, first : first + width], o_sb[:])
 
         for s in range(TOP):
-            combine(0, s)
+            combine_first(s)
         wp_bf = keep.tile([P, M, 4], BF16, align_bytes=64, name="gated0")
         nc.scalar.copy(wp_bf[:], wp_raw[:].rearrange("q r f -> q f r"))
         nc.vector.quantize_mx(out=wq[:].bitcast(FP8X4), scales=wq_s[:], in_=wp_bf[:].rearrange("q f r -> q (f r)"))
-        combine(1, 0)
-        project(0, (0, 1), 4)
+        combine_second(0)
+        c_first = keep.tile([P, HALF, 4], BF16, align_bytes=64, name="c_bf0")
+        for tb in range(TB):
+            nc.scalar.copy(c_first[:, P * tb : P * (tb + 1), :], csum[tb][:].rearrange("q r t -> q t r"))
+        project(c_first, 0, 2)
         for s in range(1, TOP):
-            combine(1, s)
-        project(1, (0,), 5)
-        project(1, (1,), 4)
+            combine_second(s)
+        c_second = []
+        for tb in range(TB):
+            pairs = held[tb][:].bitcast(F32)
+            back = psum.tile([P, 2, P], F32, name="back%d" % tb, offset=(4 + 3 * tb) * BANK)
+            for v in range(2):
+                nc.tensor.transpose(back[:, v, :], pairs[:, v : 2 * P : 2], ident[:])
+            c_bf = keep.tile([P, P, 4], BF16, align_bytes=64, name="c_second%d" % tb)
+            nc.scalar.copy(c_bf[:].bitcast(F32), back[:].rearrange("q v t -> q t v"))
+            c_second.append(c_bf)
+        for tb in range(TB):
+            project(c_second[tb], HALF + P * tb, 3 - tb)

@@ -6,7 +6,9 @@ from concourse.masks import make_identity
 K, T, E, C, N, M, TOP = 512, 512, 6, 256, 512, 128, 3
 S = E * C
 FLOPS = 2 * K * N * S + 2 * N * M * T
-BYTES = K * T + 16 * T + E * (K * N // 2 + 16 * N) + 4 * N * E + 4 * N * M + 4 * TOP * T + 2 * 128 * (S + TOP * T) // 16 + 4 * M * T
+BYTES = (
+    K * T + K * T // 32 + E * (K * N // 2 + K * N // 32) + 4 * (N * E + N * M + TOP * T + M * T) + 16 * (S + TOP * T)
+)
 
 F32 = mybir.dt.float32
 BF16 = mybir.dt.bfloat16
@@ -20,13 +22,26 @@ ACT = mybir.ActivationFunctionType
 ALU = mybir.AluOpType
 
 P = 128
+PACK = 4
+QUAD = 32
+PER_COL = 16
 NB = N // P
 HALF = T // 2
 TB = HALF // P
-BANK = 2048
-ORDER = [(e, j) for e in range(E - 2) for j in range(NB)] + [(4, 0), (4, 1), (5, 0), (5, 1), (4, 2), (5, 2), (4, 3), (5, 3)]
-ON_VECTOR = ((4, 0), (4, 1), (5, 0))
-W_GROUPS = ((0, 1), (1, 3), (3, 6))
+STAGES = 2 * TOP
+BANK, BANKS = 2048, 8
+
+W_GROUPS = ((0, 1), (1, 3), (3, E))
+WORD_RING = 4
+E_A, E_B = E - 2, E - 1
+ORDER = (
+    [(e, j) for e in range(E_A) for j in range(NB)]
+    + [(e, j) for e in (E_A, E_B) for j in range(NB // 2)]
+    + [(e, j) for j in range(NB // 2, NB) for e in (E_A, E_B)]
+)
+ON_VECTOR = ORDER[E_A * NB : E_A * NB + 3]
+TURN_BANKS = (5, 0)
+SUM_BANKS = ((2, 3), (4, 7))
 
 
 def tile_moe_nxt_lin_relu_kernel(
@@ -35,71 +50,65 @@ def tile_moe_nxt_lin_relu_kernel(
     nc = tc.nc
     with ExitStack() as ctx:
         keep = ctx.enter_context(tc.tile_pool(name="keep", bufs=1))
-        ring = ctx.enter_context(tc.tile_pool(name="ring", bufs=2))
+        ring = ctx.enter_context(tc.tile_pool(name="ring", bufs=WORD_RING))
         psum = ctx.enter_context(tc.psum_pool(name="psum", bufs=1))
 
         xw = keep.tile([P, T], I32, align_bytes=64)
-        offs_sb = keep.tile([P, S // 16], U16)
+        offs_sb = keep.tile([P, S // PER_COL], U16)
         xs = keep.tile([P, T], U8, align_bytes=64)
         ws = keep.tile([P, E, N], U8, align_bytes=64)
         w_sb = [
             keep.tile([P, stop - first, 2 * N], U8, align_bytes=64, name="w%d" % first) for first, stop in W_GROUPS
         ]
         b_sb = keep.tile([P, NB, E], F32)
-        wp_raw = keep.tile([P, 4, M], F32)
+        wp_raw = keep.tile([P, PACK, M], F32)
         g_sb = keep.tile([P, TOP * T // P], F32)
-        pos_sb = [keep.tile([P, T // 16], U16, name="pos%d" % s) for s in range(TOP)]
+        pos_sb = [keep.tile([P, T // PER_COL], U16, name="pos%d" % s) for s in range(TOP)]
         ident = keep.tile([P, P], F32)
-        warm = keep.tile([P, 2], F32)
 
         nc.vector.memset(xs[:].bitcast(I32), 0)
-        nc.vector.memset(warm[:], 0.0)
         nc.vector.memset(ws[:].rearrange("p e n -> p (e n)").bitcast(I32), 0)
-        nc.scalar.activation(warm[:, 1:2], warm[:, 0:1], ACT.Relu)
-
-        def load_words(g):
-            first, stop = W_GROUPS[g]
-            nc.sync.dma_start(w_sb[g][:].bitcast(I32), w_words[first:stop, 0].rearrange("e p c -> p e c").bitcast(I32))
 
         nc.sync.dma_start(offs_sb[:], offs)
         nc.sync.dma_start(xw[:], x_words[0].rearrange("p t r -> p (t r)").bitcast(I32))
-        for r in range(4):
-            nc.sync.dma_start(xs[r:P:32, :].bitcast(I32), x_scales[0, r:16:4, :].bitcast(I32))
-        load_words(0)
-        for r in range(4):
-            nc.sync.dma_start(
-                ws[r:P:32, :, :].bitcast(I32),
-                w_scales[:, 0, r:16:4, :].rearrange("e q n -> q e n").bitcast(I32),
-            )
+        for r in range(PACK):
+            nc.sync.dma_start(xs[r:P:QUAD, :].bitcast(I32), x_scales[0, r : K // 32 : PACK, :].bitcast(I32))
         nc.sync.dma_start(b_sb[:], b.rearrange("(j m) e -> m j e", m=P))
-        load_words(1)
-        load_words(2)
+        for r in range(PACK):
+            nc.sync.dma_start(
+                ws[r:P:QUAD, :, :].bitcast(I32),
+                w_scales[:, 0, r : K // 32 : PACK, :].rearrange("e q n -> q e n").bitcast(I32),
+            )
+        for words, (first, stop) in zip(w_sb, W_GROUPS):
+            nc.sync.dma_start(words[:].bitcast(I32), w_words[first:stop, 0].rearrange("e p c -> p e c").bitcast(I32))
         for s, pos in enumerate((pos1, pos2, pos3)):
             nc.sync.dma_start(pos_sb[s][:], pos)
-        nc.sync.dma_start(wp_raw[:], wp.rearrange("(q r) f -> q r f", r=4))
-        gate_rows = gate.rearrange("s n (u p) -> (s n u) p", p=P)
+        nc.sync.dma_start(wp_raw[:], wp.rearrange("(q r) f -> q r f", r=PACK))
+        gate_runs = gate.rearrange("s n (a p) -> (s n a) p", p=P)
+        run_step = N + 1
         with nc.allow_non_contiguous_dma(reason="one gate value a partition"):
-            nc.sync.dma_start(g_sb[:], gate_rows[0 : 11 * 513 + 1 : 513, :].rearrange("u p -> p u"))
+            nc.sync.dma_start(
+                g_sb[:], gate_runs[0 : (TOP * T // P - 1) * run_step + 1 : run_step, :].rearrange("u p -> p u")
+            )
         make_identity(nc, ident[:])
 
         xsg = keep.tile([P, S], U8, align_bytes=64)
         y = [keep.tile([P, S], F32, name="y%d" % j) for j in range(NB)]
         xg = {}
-        z = {}
 
         def gather_tokens(e):
-            picks = offs_sb[:, e * C // 16 : (e + 1) * C // 16]
-            xg[e] = ring.tile([P, C], U32, align_bytes=64, name="xg", bufs=4)
+            picks = offs_sb[:, e * C // PER_COL : (e + 1) * C // PER_COL]
+            xg[e] = ring.tile([P, C], U32, align_bytes=64, name="xg")
             nc.vector.tensor_copy(xg[e][:], xw[:].bitcast(U32).indirect(picks))
             nc.vector.tensor_copy(xsg[:, e * C : (e + 1) * C], xs[:].indirect(picks))
 
-        def expert_block(e, j):
+        def expert_product(e, j):
             slots = slice(e * C, (e + 1) * C)
-            g = [first <= e < stop for first, stop in W_GROUPS].index(True)
-            words = w_sb[g][:, e - W_GROUPS[g][0], :]
-            z[e, j] = psum.tile([P, C], F32, name="z%d_%d" % (e, j), offset=(ORDER.index((e, j)) % 8) * BANK)
+            group = [first <= e < stop for first, stop in W_GROUPS].index(True)
+            words = w_sb[group][:, e - W_GROUPS[group][0], :]
+            z = psum.tile([P, C], F32, name="z%d_%d" % (e, j), offset=(ORDER.index((e, j)) % BANKS) * BANK)
             nc.tensor.matmul_mx(
-                out=z[e, j][:],
+                out=z[:],
                 lhsT=words[:, 2 * P * j : 2 * P * (j + 1)].bitcast(FP4X4),
                 lhsT_scale=ws[:, e, P * j : P * (j + 1)],
                 rhs=xg[e][:].bitcast(FP8X4),
@@ -107,109 +116,92 @@ def tile_moe_nxt_lin_relu_kernel(
                 start=True,
                 stop=True,
             )
-
-        def finish_block(e, j):
-            slots = slice(e * C, (e + 1) * C)
+            bias = b_sb[:, j, e : e + 1]
             if (e, j) in ON_VECTOR:
-                nc.vector.tensor_scalar(y[j][:, slots], z[e, j][:], b_sb[:, j, e : e + 1], 0.0, ALU.add, ALU.max)
+                nc.vector.tensor_scalar(y[j][:, slots], z[:], bias, 0.0, ALU.add, ALU.max)
             else:
-                nc.scalar.activation(y[j][:, slots], z[e, j][:], ACT.Relu, bias=b_sb[:, j, e : e + 1])
+                nc.scalar.activation(y[j][:, slots], z[:], ACT.Relu, bias=bias)
 
         for e, j in ORDER:
-            if j == 0 and e < E - 1:
+            if j == 0 and e < E_B:
                 gather_tokens(e)
-            if (e, j) == (E - 2, 0):
-                gather_tokens(E - 1)
-            expert_block(e, j)
-            finish_block(e, j)
+            if (e, j) == (E_A, 0):
+                gather_tokens(E_B)
+            expert_product(e, j)
 
         wq = keep.tile([P, M], U32, align_bytes=64)
         wq_s = keep.tile([P, M], U8, align_bytes=64)
-
-        csum = [psum.tile([P, 4, P], F32, name="csum%d" % tb, offset=(2 + tb) * BANK) for tb in range(TB)]
+        csum = {}
         held = {}
 
-        def fetch(h, s):
-            picks = pos_sb[s][:, h * HALF // 16 : (h + 1) * HALF // 16]
+        def combine(h, s):
+            if s == 0:
+                for tb in range(TB):
+                    bank = SUM_BANKS[h][tb]
+                    csum[h, tb] = psum.tile([P, PACK, P], F32, name="csum%d" % bank, offset=bank * BANK)
+            picks = pos_sb[s][:, h * HALF // PER_COL : (h + 1) * HALF // PER_COL]
             stage = TOP * h + s
-            turned = psum.tile([P, TB, N], F32, name="turned%d" % stage, offset=(0 if stage % 2 else 5) * BANK)
+            turned = psum.tile([P, TB, N], F32, name="turned%d" % stage, offset=TURN_BANKS[stage % 2] * BANK)
             for j in range(NB):
-                if stage == 2 * TOP - 1 and j == 2:
-                    got = keep.tile([P, HALF], F32, align_bytes=64, name="c_bf0")
-                else:
-                    got = keep.tile([P, HALF], F32, name="got%d" % j)
+                got = keep.tile([P, HALF], F32, name="got%d" % j)
                 nc.vector.tensor_copy(got[:], y[j][:].indirect(picks))
                 for tb in range(TB):
                     nc.tensor.transpose(turned[:, tb, P * j : P * (j + 1)], got[:, P * tb : P * (tb + 1)], ident[:])
-            return turned
-
-        def combine_first(s):
-            turned = fetch(0, s)
             for tb in range(TB):
-                u = 4 * s + tb
-                gated = keep.tile([P, 4, P], F32, align_bytes=64, name="gated%d" % u)
-                view = turned[:, tb, :].rearrange("t (q r) -> t r q", r=4)
-                nc.scalar.activation(gated[:], view, ACT.Copy, scale=g_sb[:, u : u + 1])
-                for r in range(4):
-                    nc.tensor.matmul(
-                        csum[tb][:, r, :],
-                        lhsT=gated[:, r, :],
-                        rhs=ident[:],
-                        is_transpose=True,
-                        start=(s == 0 and r == 0),
-                        stop=(s == TOP - 1 and r == 3),
-                    )
-
-        def combine_second(s):
-            turned = fetch(1, s)
-            for tb in range(TB):
-                u = 4 * s + TB + tb
-                part = keep.tile([P, N], BF16 if s == TOP - 1 else F32, name="part%d" % u)
-                if s == 0:
-                    nc.scalar.activation(part[:], turned[:, tb, :], ACT.Copy, scale=g_sb[:, u : u + 1])
+                u = (T // P) * s + TB * h + tb
+                gated = keep.tile([P, PACK, P], F32, align_bytes=64, name="gated%d" % u)
+                weight = g_sb[:, u : u + 1]
+                view = turned[:, tb, :].rearrange("t (q r) -> t r q", r=PACK)
+                if stage == STAGES - 1:
+                    nc.vector.scalar_tensor_tensor(gated[:], view, weight, held[tb][:], ALU.mult, ALU.add)
                 else:
-                    nc.vector.scalar_tensor_tensor(
-                        part[:], turned[:, tb, :], g_sb[:, u : u + 1], held[tb][:], ALU.mult, ALU.add
-                    )
-                held[tb] = part
+                    nc.scalar.activation(gated[:], view, ACT.Copy, scale=weight)
+                if stage == STAGES - 2:
+                    held[tb] = gated
+                else:
+                    for r in range(PACK):
+                        nc.tensor.matmul(
+                            csum[h, tb][:, r, :],
+                            lhsT=gated[:, r, :],
+                            rhs=ident[:],
+                            is_transpose=True,
+                            start=(s == 0 and r == 0),
+                            stop=(s == TOP - 1 and r == PACK - 1),
+                        )
 
-        def project(c_bf, first, bank):
-            width = c_bf.shape[1]
+        def project(h, blocks, bank):
+            first, width = HALF * h + P * blocks[0], P * len(blocks)
+            c_bf = keep.tile([P, width, PACK], BF16, align_bytes=64, name="c_bf%d" % first)
+            for i, tb in enumerate(blocks):
+                nc.scalar.copy(c_bf[:, P * i : P * (i + 1), :], csum[h, tb][:].rearrange("q r t -> q t r"))
             cq = keep.tile([P, width], U32, align_bytes=64, name="cq%d" % first)
             cq_s = keep.tile([P, width], U8, align_bytes=64, name="cq_s%d" % first)
             nc.vector.quantize_mx(out=cq[:].bitcast(FP8X4), scales=cq_s[:], in_=c_bf[:].rearrange("q t r -> q (t r)"))
             proj = psum.tile([P, width], F32, name="proj%d" % first, offset=bank * BANK)
             nc.tensor.matmul_mx(
-                out=proj[:], lhsT=wq[:].bitcast(FP8X4), lhsT_scale=wq_s[:], rhs=cq[:].bitcast(FP8X4), rhs_scale=cq_s[:],
-                start=True, stop=True,
+                out=proj[:],
+                lhsT=wq[:].bitcast(FP8X4),
+                lhsT_scale=wq_s[:],
+                rhs=cq[:].bitcast(FP8X4),
+                rhs_scale=cq_s[:],
+                start=True,
+                stop=True,
             )
             o_sb = keep.tile([P, width], F32, name="o_sb%d" % first)
-            if first == T - P:
+            if first + width == T:
                 nc.vector.tensor_copy(o_sb[:], proj[:])
             else:
                 nc.scalar.copy(o_sb[:], proj[:])
             nc.sync.dma_start(out[:, first : first + width], o_sb[:])
 
         for s in range(TOP):
-            combine_first(s)
-        wp_bf = keep.tile([P, M, 4], BF16, align_bytes=64, name="gated0")
+            combine(0, s)
+        wp_bf = keep.tile([P, M, PACK], BF16, align_bytes=64, name="gated0")
         nc.scalar.copy(wp_bf[:], wp_raw[:].rearrange("q r f -> q f r"))
         nc.vector.quantize_mx(out=wq[:].bitcast(FP8X4), scales=wq_s[:], in_=wp_bf[:].rearrange("q f r -> q (f r)"))
-        combine_second(0)
-        c_first = keep.tile([P, HALF, 4], BF16, align_bytes=64, name="c_bf0")
-        for tb in range(TB):
-            nc.scalar.copy(c_first[:, P * tb : P * (tb + 1), :], csum[tb][:].rearrange("q r t -> q t r"))
-        project(c_first, 0, 2)
+        combine(1, 0)
+        project(0, (0, 1), SUM_BANKS[0][0])
         for s in range(1, TOP):
-            combine_second(s)
-        c_second = []
-        for tb in range(TB):
-            pairs = held[tb][:].bitcast(F32)
-            back = psum.tile([P, 2, P], F32, name="back%d" % tb, offset=(4 + 3 * tb) * BANK)
-            for v in range(2):
-                nc.tensor.transpose(back[:, v, :], pairs[:, v : 2 * P : 2], ident[:])
-            c_bf = keep.tile([P, P, 4], BF16, align_bytes=64, name="c_second%d" % tb)
-            nc.scalar.copy(c_bf[:].bitcast(F32), back[:].rearrange("q v t -> q t v"))
-            c_second.append(c_bf)
-        for tb in range(TB):
-            project(c_second[tb], HALF + P * tb, 3 - tb)
+            combine(1, s)
+        project(1, (0,), SUM_BANKS[0][1])
+        project(1, (1,), SUM_BANKS[0][0])

from contextlib import ExitStack

import concourse.mybir as mybir
from concourse.masks import make_identity

K, T, E, C, N, M, TOP = 512, 512, 6, 256, 512, 128, 3
S = E * C
FLOPS = 2 * K * N * S + 2 * N * M * T
BYTES = (
    K * T + K * T // 32 + E * (K * N // 2 + K * N // 32) + 4 * (N * E + N * M + TOP * T + M * T) + 16 * (S + TOP * T)
)

F32 = mybir.dt.float32
BF16 = mybir.dt.bfloat16
I32 = mybir.dt.int32
U32 = mybir.dt.uint32
U16 = mybir.dt.uint16
U8 = mybir.dt.uint8
FP8X4 = mybir.dt.float8_e4m3fn_x4
FP4X4 = mybir.dt.float4_e2m1fn_x4
ACT = mybir.ActivationFunctionType
ALU = mybir.AluOpType

P = 128
PACK = 4
QUAD = 32
PER_COL = 16
NB = N // P
HALF = T // 2
TB = HALF // P
STAGES = 2 * TOP
BANK, BANKS = 2048, 8

W_GROUPS = ((0, 1), (1, 3), (3, E))
WORD_RING = 4
E_A, E_B = E - 2, E - 1
ORDER = (
    [(e, j) for e in range(E_A) for j in range(NB)]
    + [(e, j) for e in (E_A, E_B) for j in range(NB // 2)]
    + [(e, j) for j in range(NB // 2, NB) for e in (E_A, E_B)]
)
ON_VECTOR = ORDER[E_A * NB : E_A * NB + 3]
TURN_BANKS = (5, 0)
SUM_BANKS = ((2, 3), (4, 7))


def tile_moe_nxt_lin_relu_kernel(
    tc, x_words, x_scales, w_words, w_scales, b, wp, gate, offs, pos1, pos2, pos3, out
):
    nc = tc.nc
    with ExitStack() as ctx:
        keep = ctx.enter_context(tc.tile_pool(name="keep", bufs=1))
        ring = ctx.enter_context(tc.tile_pool(name="ring", bufs=WORD_RING))
        psum = ctx.enter_context(tc.psum_pool(name="psum", bufs=1))

        xw = keep.tile([P, T], I32, align_bytes=64)
        offs_sb = keep.tile([P, S // PER_COL], U16)
        xs = keep.tile([P, T], U8, align_bytes=64)
        ws = keep.tile([P, E, N], U8, align_bytes=64)
        w_sb = [
            keep.tile([P, stop - first, 2 * N], U8, align_bytes=64, name="w%d" % first) for first, stop in W_GROUPS
        ]
        b_sb = keep.tile([P, NB, E], F32)
        wp_raw = keep.tile([P, PACK, M], F32)
        g_sb = keep.tile([P, TOP * T // P], F32)
        pos_sb = [keep.tile([P, T // PER_COL], U16, name="pos%d" % s) for s in range(TOP)]
        ident = keep.tile([P, P], F32)

        nc.vector.memset(xs[:].bitcast(I32), 0)
        nc.vector.memset(ws[:].rearrange("p e n -> p (e n)").bitcast(I32), 0)

        nc.sync.dma_start(offs_sb[:], offs)
        nc.sync.dma_start(xw[:], x_words[0].rearrange("p t r -> p (t r)").bitcast(I32))
        for r in range(PACK):
            nc.sync.dma_start(xs[r:P:QUAD, :].bitcast(I32), x_scales[0, r : K // 32 : PACK, :].bitcast(I32))
        nc.sync.dma_start(b_sb[:], b.rearrange("(j m) e -> m j e", m=P))
        for r in range(PACK):
            nc.sync.dma_start(
                ws[r:P:QUAD, :, :].bitcast(I32),
                w_scales[:, 0, r : K // 32 : PACK, :].rearrange("e q n -> q e n").bitcast(I32),
            )
        for words, (first, stop) in zip(w_sb, W_GROUPS):
            nc.sync.dma_start(words[:].bitcast(I32), w_words[first:stop, 0].rearrange("e p c -> p e c").bitcast(I32))
        for s, pos in enumerate((pos1, pos2, pos3)):
            nc.sync.dma_start(pos_sb[s][:], pos)
        nc.sync.dma_start(wp_raw[:], wp.rearrange("(q r) f -> q r f", r=PACK))
        gate_runs = gate.rearrange("s n (a p) -> (s n a) p", p=P)
        run_step = N + 1
        with nc.allow_non_contiguous_dma(reason="one gate value a partition"):
            nc.sync.dma_start(
                g_sb[:], gate_runs[0 : (TOP * T // P - 1) * run_step + 1 : run_step, :].rearrange("u p -> p u")
            )
        make_identity(nc, ident[:])

        xsg = keep.tile([P, S], U8, align_bytes=64)
        y = [keep.tile([P, S], F32, name="y%d" % j) for j in range(NB)]
        xg = {}

        def gather_tokens(e):
            picks = offs_sb[:, e * C // PER_COL : (e + 1) * C // PER_COL]
            xg[e] = ring.tile([P, C], U32, align_bytes=64, name="xg")
            nc.vector.tensor_copy(xg[e][:], xw[:].bitcast(U32).indirect(picks))
            nc.vector.tensor_copy(xsg[:, e * C : (e + 1) * C], xs[:].indirect(picks))

        def expert_product(e, j):
            slots = slice(e * C, (e + 1) * C)
            group = [first <= e < stop for first, stop in W_GROUPS].index(True)
            words = w_sb[group][:, e - W_GROUPS[group][0], :]
            z = psum.tile([P, C], F32, name="z%d_%d" % (e, j), offset=(ORDER.index((e, j)) % BANKS) * BANK)
            nc.tensor.matmul_mx(
                out=z[:],
                lhsT=words[:, 2 * P * j : 2 * P * (j + 1)].bitcast(FP4X4),
                lhsT_scale=ws[:, e, P * j : P * (j + 1)],
                rhs=xg[e][:].bitcast(FP8X4),
                rhs_scale=xsg[:, slots],
                start=True,
                stop=True,
            )
            bias = b_sb[:, j, e : e + 1]
            if (e, j) in ON_VECTOR:
                nc.vector.tensor_scalar(y[j][:, slots], z[:], bias, 0.0, ALU.add, ALU.max)
            else:
                nc.scalar.activation(y[j][:, slots], z[:], ACT.Relu, bias=bias)

        for e, j in ORDER:
            if j == 0 and e < E_B:
                gather_tokens(e)
            if (e, j) == (E_A, 0):
                gather_tokens(E_B)
            expert_product(e, j)

        wq = keep.tile([P, M], U32, align_bytes=64)
        wq_s = keep.tile([P, M], U8, align_bytes=64)
        csum = {}
        held = {}

        def combine(h, s):
            if s == 0:
                for tb in range(TB):
                    bank = SUM_BANKS[h][tb]
                    csum[h, tb] = psum.tile([P, PACK, P], F32, name="csum%d" % bank, offset=bank * BANK)
            picks = pos_sb[s][:, h * HALF // PER_COL : (h + 1) * HALF // PER_COL]
            stage = TOP * h + s
            turned = psum.tile([P, TB, N], F32, name="turned%d" % stage, offset=TURN_BANKS[stage % 2] * BANK)
            for j in range(NB):
                got = keep.tile([P, HALF], F32, name="got%d" % j)
                nc.vector.tensor_copy(got[:], y[j][:].indirect(picks))
                for tb in range(TB):
                    nc.tensor.transpose(turned[:, tb, P * j : P * (j + 1)], got[:, P * tb : P * (tb + 1)], ident[:])
            for tb in range(TB):
                u = (T // P) * s + TB * h + tb
                gated = keep.tile([P, PACK, P], F32, align_bytes=64, name="gated%d" % u)
                weight = g_sb[:, u : u + 1]
                view = turned[:, tb, :].rearrange("t (q r) -> t r q", r=PACK)
                if stage == STAGES - 1:
                    nc.vector.scalar_tensor_tensor(gated[:], view, weight, held[tb][:], ALU.mult, ALU.add)
                else:
                    nc.scalar.activation(gated[:], view, ACT.Copy, scale=weight)
                if stage == STAGES - 2:
                    held[tb] = gated
                else:
                    for r in range(PACK):
                        nc.tensor.matmul(
                            csum[h, tb][:, r, :],
                            lhsT=gated[:, r, :],
                            rhs=ident[:],
                            is_transpose=True,
                            start=(s == 0 and r == 0),
                            stop=(s == TOP - 1 and r == PACK - 1),
                        )

        def project(h, blocks, bank):
            first, width = HALF * h + P * blocks[0], P * len(blocks)
            c_bf = keep.tile([P, width, PACK], BF16, align_bytes=64, name="c_bf%d" % first)
            for i, tb in enumerate(blocks):
                nc.scalar.copy(c_bf[:, P * i : P * (i + 1), :], csum[h, tb][:].rearrange("q r t -> q t r"))
            cq = keep.tile([P, width], U32, align_bytes=64, name="cq%d" % first)
            cq_s = keep.tile([P, width], U8, align_bytes=64, name="cq_s%d" % first)
            nc.vector.quantize_mx(out=cq[:].bitcast(FP8X4), scales=cq_s[:], in_=c_bf[:].rearrange("q t r -> q (t r)"))
            proj = psum.tile([P, width], F32, name="proj%d" % first, offset=bank * BANK)
            nc.tensor.matmul_mx(
                out=proj[:],
                lhsT=wq[:].bitcast(FP8X4),
                lhsT_scale=wq_s[:],
                rhs=cq[:].bitcast(FP8X4),
                rhs_scale=cq_s[:],
                start=True,
                stop=True,
            )
            o_sb = keep.tile([P, width], F32, name="o_sb%d" % first)
            if first + width == T:
                nc.vector.tensor_copy(o_sb[:], proj[:])
            else:
                nc.scalar.copy(o_sb[:], proj[:])
            nc.sync.dma_start(out[:, first : first + width], o_sb[:])

        for s in range(TOP):
            combine(0, s)
        wp_bf = keep.tile([P, M, PACK], BF16, align_bytes=64, name="gated0")
        nc.scalar.copy(wp_bf[:], wp_raw[:].rearrange("q r f -> q f r"))
        nc.vector.quantize_mx(out=wq[:].bitcast(FP8X4), scales=wq_s[:], in_=wp_bf[:].rearrange("q f r -> q (f r)"))
        combine(1, 0)
        project(0, (0, 1), SUM_BANKS[0][0])
        for s in range(1, TOP):
            combine(1, s)
        project(1, (0,), SUM_BANKS[0][1])
        project(1, (1,), SUM_BANKS[0][0])
